import numpy as np, ml_dtypes
CORES = [23,119,17,113]
N = 4
import mx_ref
NC = 128
BF = ml_dtypes.bfloat16
def cut(t, i, w=512):
    return t[:, w * i:w * i + w]
def tile(rs):
    return np.stack(rs, axis=2).reshape(128, -1).astype(BF)
def onehot(t, r):
    own, p, b = t[:, :NC], t[:, NC:2 * NC], t[:, 2 * NC:]
    return tile([((own == r) & (p == np.arange(128)[:, None]) & (b == f)).astype(np.float32) for f in range(4)])
def setup_inputs(rng):
    def f(*shape):
        return mx_ref.flush((rng.standard_normal(shape, dtype=np.float32) * np.exp2(rng.integers(-2, 3, shape[:-1] + (1,)))).astype(BF))
    t = np.concatenate([rng.integers(0, N, (N, 1, NC)), rng.integers(0, 128, (N, 1, NC)), rng.integers(0, 4, (N, 1, NC))], axis=2)
    return {"tg": np.broadcast_to(t, (N, 128, 3 * NC)).astype(BF).copy(), "tab": f(N, 128, 4 * 512), "w": f(N, 128, 512)}
def setup_inputs_blocks(rng):
    d = setup_inputs(rng)
    for k in ("tab", "w"): d[k] = mx_ref.spread(d[k], rng, 4)
    return d
def setup_inputs_wide(rng):
    d = setup_inputs(rng)
    for k in ("tab", "w"): d[k] = mx_ref.flush((d[k].astype(np.float32) * np.exp2(rng.integers(-6, 7, (N, 1, 1))).astype(np.float32)).astype(BF))
    return d
def setup_inputs_hot(rng):
    d = setup_inputs(rng); t = d["tg"].astype(np.float32); t[:, :, :NC] = rng.integers(0, N); t[:, :, NC:2 * NC] = np.broadcast_to(rng.integers(0, 4, (N, 1, NC)), (N, 128, NC))
    d["tg"] = t.astype(BF)
    return d
def reference(tg, tab, w):
    y = np.zeros((N, 128, NC), np.float32)
    for j in range(N):
        qw = mx_ref.quantize(w[j])
        for r in range(N):
            o = mx_ref.quantize(onehot(tg[j].astype(np.float32), r))
            e = mx_ref.quantize(tile([mx_ref.matmul(mx_ref.quantize(cut(tab[r], f)), o) for f in range(4)]))
            p = mx_ref.matmul(qw, e)
            y[j] = p if r == 0 else y[j] + p
    return {"y": y}

@@ -1,0 +1,216 @@
+from concourse.bass import DstId, RemoteDMATransfer
+from concourse.mybir import dt, AluOpType, ActivationFunctionType
+
+NC = 128
+SCRATCH = {
+    "idc": ("sbuf", [128, 3], "bfloat16"),
+    "idl": ("sbuf", [128, 9], "bfloat16"),
+    "tgf": ("sbuf", [128, 384], "bfloat16"),
+    "tabf": ("sbuf", [128, 2048], "bfloat16"),
+    "wf": ("sbuf", [128, 512], "bfloat16"),
+    "tabq": ("sbuf", [128, 512], "float8_e4m3fn_x4"),
+    "tabs": ("sbuf", [128, 512], "uint8"),
+    "wq": ("sbuf", [128, 128], "float8_e4m3fn_x4"),
+    "ws": ("sbuf", [128, 128], "uint8"),
+    "vb": ("sbuf", [128, 4], "bfloat16"),
+    "zero": ("sbuf", [128, 32], "bfloat16"),
+    "ka": ("sbuf", [128, 128], "float32"),
+    "kb": ("sbuf", [128, 128], "float32"),
+    "kc": ("sbuf", [128, 128], "float32"),
+    "kown": ("sbuf", [128, 128], "bfloat16"),
+    "u": ("sbuf", [128, 3], "float32"),
+    "v": ("sbuf", [128, 3], "float32"),
+    "x": ("sbuf", [128, 96], "bfloat16"),
+    "xt": ("sbuf", [128, 96], "bfloat16"),
+    "key": ("sbuf", [128, 384], "bfloat16"),
+    "of": ("sbuf", [128, 2048], "bfloat16"),
+    "oq": ("sbuf", [128, 512], "float8_e4m3fn_x4"),
+    "osc": ("sbuf", [128, 512], "uint8"),
+    "ef": ("sbuf", [128, 2048], "bfloat16"),
+    "eq": ("sbuf", [128, 512], "float8_e4m3fn_x4"),
+    "esc": ("sbuf", [128, 512], "uint8"),
+    "rq": ("sbuf", [128, 384], "float8_e4m3fn_x4"),
+    "rs": ("sbuf", [128, 384], "uint8"),
+    "yo": ("sbuf", [128, 128], "float32"),
+    "ps": ("psum", [128, 4096], "float32"),
+}
+SEMAPHORES = (["idload", "tgload", "tabload", "wload", "ystore", "idarr", "sent", "iot", "fill",
+               "k1", "k2", "k3", "tabdone", "wdone", "r1", "r2", "r3", "r4", "yp", "yv"]
+              + ["arr%d" % s for s in range(3)]
+              + ["cmp%d" % s for s in range(4)] + ["qo%d" % s for s in range(4)]
+              + ["ev%d" % s for s in range(4)] + ["qe%d" % s for s in range(4)]
+              + ["z%d%d" % (s, f) for s in range(4) for f in range(4)])
+
+
+def _bits(m):
+    return [i for i in range(m.bit_length()) if (m >> i) & 1]
+
+
+def _mask(b):
+    return sum(1 << i for i in b)
+
+
+def _peers(cores, me, topo):
+    def far(j):
+        return (topo.chip(cores[j]) == topo.chip(cores[me]), topo.die(cores[j]) == topo.die(cores[me]), j)
+    return sorted([j for j in range(len(cores)) if j != me], key=far)
+
+
+def rank_program(g, core, T, topo):
+    rank = T.rank_of(core)
+    if rank is None:
+        return
+    cores = T.cores
+    S = T.sem
+    A = AluOpType
+    COPY = ActivationFunctionType.Copy
+    peers = _peers(cores, rank, topo)
+    dst = [cores[j] for j in peers]
+    slot = [_peers(cores, j, topo).index(rank) for j in peers]
+    off_bits = _bits(topo.mask(core, dst[0]))
+    on_bits = [b for b in _bits(topo.mask(core, dst[2])) if b not in off_bits]
+    half = len(off_bits) // 2
+
+    def did(k):
+        rid, pid, _ = topo.addr(dst[k])
+        return DstId(rid=rid, pnc=pid)
+
+    off = -float(1024 * rank + 256)
+
+    g.sync.dma_start(T.idc[:, 0:1], T.tg[0:1, 0:NC]).then_inc(S.idload, 16)
+    g.scalar.dma_start(T.idc[:, 1:2], T.tg[0:1, NC:2 * NC]).then_inc(S.idload, 16)
+    g.sync.dma_start(T.idc[:, 2:3], T.tg[0:1, 2 * NC:3 * NC]).then_inc(S.idload, 16)
+    g.scalar.dma_start(T.tgf[:, :], T.tg[:, :]).then_inc(S.tgload, 16)
+    g.sync.dma_start(T.tabf[:, :], T.tab[:, :]).then_inc(S.tabload, 16)
+    g.scalar.dma_start(T.wf[:, :], T.w[:, :]).then_inc(S.wload, 16)
+
+    g.iota(T.vb[:, :], [[1, 4]], -256, 4, allow_small_or_imprecise_dtypes=True).then_inc(S.iot, 1)
+    g.wait_ge(S.idload, 48)
+    idm = [off_bits[:half], off_bits[half:], on_bits[:half]]
+    g.remote_dma_fused(
+        [RemoteDMATransfer(dst_ids=[did(k)], dma_engine_mask=_mask(idm[k]), remote_sem=S.idarr,
+                           src=T.idc[:, 0:3], dst=T.idl[:, 3 * slot[k]:3 * slot[k] + 3]) for k in range(3)],
+        local_sem=S.sent)
+    sent = sum(len(m) for m in idm)
+
+    V = g.vector
+    V.memset(T.zero[:, :], 0.0).then_inc(S.fill, 1)
+    V.wait_ge(S.tgload, 16)
+    V.tensor_scalar(T.ka[:, :], T.tgf[:, 0:NC], 1024.0, off, A.mult, A.add).then_inc(S.k1, 1)
+    V.tensor_scalar(T.kb[:, :], T.tgf[:, NC:2 * NC], 4.0, None, A.mult).then_inc(S.k1, 1)
+    V.wait_ge(S.k1, 2)
+    V.tensor_tensor(T.kc[:, :], T.ka[:, :], T.kb[:, :], A.add).then_inc(S.k2, 1)
+    V.wait_ge(S.k2, 1)
+    V.tensor_tensor(T.kown[:, :], T.kc[:, :], T.tgf[:, 2 * NC:3 * NC], A.add).then_inc(S.k3, 1)
+    V.wait_ge(S.k3, 1)
+    V.wait_ge(S.iot, 1)
+
+    def onehot(s, keys):
+        for b in range(4):
+            V.tensor_scalar(T.of[:, 512 * s + b:512 * s + 512:4], keys, T.vb[:, b:b + 1], None,
+                            A.is_equal).then_inc(S["cmp%d" % s], 1)
+        V.wait_ge(S["cmp%d" % s], 4)
+        V.quantize_mx(T.oq[:, 128 * s:128 * s + 128], T.osc[:, 128 * s:128 * s + 128],
+                      T.of[:, 512 * s:512 * s + 512]).then_inc(S["qo%d" % s], 1)
+
+    onehot(3, T.kown[:, :])
+    V.wait_ge(S.tabload, 16)
+    V.quantize_mx(T.tabq[:, :], T.tabs[:, :], T.tabf[:, :]).then_inc(S.tabdone, 1)
+    V.wait_ge(S.wload, 16)
+    V.quantize_mx(T.wq[:, :], T.ws[:, :], T.wf[:, :]).then_inc(S.wdone, 1)
+
+    V.wait_ge(S.fill, 1)
+    V.wait_ge(S.idarr, sum(len(m) for m in idm))
+    V.tensor_scalar(T.u[:, :], T.idl[:, 1:9:3], 4.0, off, A.mult, A.add).then_inc(S.r1, 1)
+    for s in range(3):
+        V.tensor_scalar(T.v[:, s:s + 1], T.idl[:, 3 * s:3 * s + 1], 1024.0, T.idl[:, 3 * s + 2:3 * s + 3],
+                        A.mult, A.add).then_inc(S.r1, 1)
+    V.wait_ge(S.r1, 4)
+    for s in range(3):
+        V.tensor_scalar(T.x[:, 32 * s:32 * s + 32], T.zero[:, :], T.u[:, s:s + 1], T.v[:, s:s + 1],
+                        A.add, A.add).then_inc(S.r2, 1)
+    V.wait_ge(S.r2, 3)
+    for s in range(3):
+        V.transpose(T.xt[:, s:96:3], T.x[:, 32 * s:32 * s + 32]).then_inc(S.r3, 1)
+    V.wait_ge(S.r3, 3)
+    g.scalar.wait_ge(S.r3, 3)
+    spread = [(m, a) for m in range(4) for a in range(4)]
+    for i, (m, a) in enumerate(spread):
+        o = T.key[32 * a:32 * a + 32, 96 * m:96 * m + 96]
+        n = T.xt[32 * m:32 * m + 32, 0:96]
+        if i < 10:
+            V.tensor_copy(o, n).then_inc(S.r4, 1)
+        else:
+            g.scalar.activation(o, n, COPY).then_inc(S.r4, 1)
+    V.wait_ge(S.r4, 16)
+    for s in range(3):
+        onehot(s, T.key[:, s:384:3])
+
+    P = g.tensor
+    P.wait_ge(S.tabdone, 1)
+    order = [0, 1, 2, 3]
+    bank = {0: 0, 1: 4, 2: 0, 3: 4}
+
+    def zview(s, f):
+        c = 512 * (bank[s] + f)
+        return T.ps[:, c:c + 128]
+
+    for s in order:
+        P.wait_ge(S["qo%d" % s], 1)
+        if s >= 2:
+            P.wait_ge(S["ev%d" % (s - 2)], 4)
+        for f in range(4):
+            P.matmul_mx(zview(s, f), T.tabq[:, 128 * f:128 * f + 128], T.tabs[:, 128 * f:128 * f + 128],
+                        T.oq[:, 128 * s:128 * s + 128], T.osc[:, 128 * s:128 * s + 128],
+                        True, True).then_inc(S["z%d%d" % (s, f)], 1)
+
+    for s in order:
+        for f in range(4):
+            o = T.ef[:, 512 * s + f:512 * s + 512:4]
+            if s == 0 or f % 2 == 0:
+                g.scalar.wait_ge(S["z%d%d" % (s, f)], 1)
+                g.scalar.activation(o, zview(s, f), COPY).then_inc(S["ev%d" % s], 1)
+            else:
+                V.wait_ge(S["z%d%d" % (s, f)], 1)
+                V.tensor_copy(o, zview(s, f)).then_inc(S["ev%d" % s], 1)
+        V.wait_ge(S["ev%d" % s], 4)
+        V.quantize_mx(T.eq[:, 128 * s:128 * s + 128], T.esc[:, 128 * s:128 * s + 128],
+                      T.ef[:, 512 * s:512 * s + 512]).then_inc(S["qe%d" % s], 1)
+
+    def codes(t, k):
+        return t[:, 128 * k:128 * k + 128].bitcast(dt.uint8)
+
+    def scales(t, k):
+        return t[:, 128 * k:128 * k + 128]
+
+    em = [off_bits, off_bits, on_bits]
+    rid0, pid0, _ = topo.addr(dst[0])
+    g.wait_ge(S.qe0, 1)
+    for part, src, land in ((codes, T.eq, T.rq), (scales, T.esc, T.rs)):
+        g.remote_dma(part(land, slot[0]), part(src, 0), S["arr%d" % slot[0]], S.sent, pid0, rid0, _mask(em[0]))
+        sent += len(em[0])
+    g.wait_ge(S.qe1, 1)
+    g.wait_ge(S.qe2, 1)
+    for part, src, land in ((codes, T.eq, T.rq), (scales, T.esc, T.rs)):
+        g.remote_dma_fused(
+            [RemoteDMATransfer(dst_ids=[did(k)], dma_engine_mask=_mask(em[k]), remote_sem=S["arr%d" % slot[k]],
+                               src=part(src, k), dst=part(land, slot[k])) for k in (1, 2)],
+            local_sem=S.sent)
+        sent += len(em[1]) + len(em[2])
+    g.wait_ge(S.sent, sent)
+
+    P.wait_ge(S.wdone, 1)
+    P.wait_ge(S.qe3, 1)
+    P.wait_ge(S.ev2, 4)
+    out = T.ps[:, 0:128]
+    P.matmul_mx(out, T.wq[:, :], T.ws[:, :], T.eq[:, 384:512], T.esc[:, 384:512], True, False)
+    for i, s in enumerate((0, 2, 1)):
+        P.wait_ge(S["arr%d" % s], 2 * len(em[s]))
+        m = P.matmul_mx(out, T.wq[:, :], T.ws[:, :], T.rq[:, 128 * s:128 * s + 128], T.rs[:, 128 * s:128 * s + 128],
+                        False, i == 2)
+    m.then_inc(S.yp, 1)
+    V.wait_ge(S.yp, 1)
+    V.tensor_copy(T.yo[:, :], out).then_inc(S.yv, 1)
+    g.sync.wait_ge(S.yv, 1)
+    g.sync.dma_start(T.y[:, :], T.yo[:, :]).then_inc(S.ystore, 16)
+    g.sync.wait_ge(S.ystore, 16)

@@ -2,10 +2,12 @@ from concourse.bass import DstId, RemoteDMATransfer
 from concourse.mybir import dt, AluOpType, ActivationFunctionType
 
 NC = 128
+OWN = 3
 SCRATCH = {
-    "idc": ("sbuf", [128, 3], "bfloat16"),
-    "idl": ("sbuf", [128, 9], "bfloat16"),
-    "tgf": ("sbuf", [128, 384], "bfloat16"),
+    "idl": ("sbuf", [128, 4, 40], "bfloat16"),
+    "d0": ("sbuf", [128, 35], "bfloat16"),
+    "x": ("sbuf", [128, 4, 64], "bfloat16"),
+    "key": ("sbuf", [128, 4, 128], "bfloat16"),
     "tabf": ("sbuf", [128, 2048], "bfloat16"),
     "wf": ("sbuf", [128, 512], "bfloat16"),
     "tabq": ("sbuf", [128, 512], "float8_e4m3fn_x4"),
@@ -13,16 +15,6 @@ SCRATCH = {
     "wq": ("sbuf", [128, 128], "float8_e4m3fn_x4"),
     "ws": ("sbuf", [128, 128], "uint8"),
     "vb": ("sbuf", [128, 4], "bfloat16"),
-    "zero": ("sbuf", [128, 32], "bfloat16"),
-    "ka": ("sbuf", [128, 128], "float32"),
-    "kb": ("sbuf", [128, 128], "float32"),
-    "kc": ("sbuf", [128, 128], "float32"),
-    "kown": ("sbuf", [128, 128], "bfloat16"),
-    "u": ("sbuf", [128, 3], "float32"),
-    "v": ("sbuf", [128, 3], "float32"),
-    "x": ("sbuf", [128, 96], "bfloat16"),
-    "xt": ("sbuf", [128, 96], "bfloat16"),
-    "key": ("sbuf", [128, 384], "bfloat16"),
     "of": ("sbuf", [128, 2048], "bfloat16"),
     "oq": ("sbuf", [128, 512], "float8_e4m3fn_x4"),
     "osc": ("sbuf", [128, 512], "uint8"),
@@ -34,9 +26,10 @@ SCRATCH = {
     "yo": ("sbuf", [128, 128], "float32"),
     "ps": ("psum", [128, 4096], "float32"),
 }
-SEMAPHORES = (["idload", "tgload", "tabload", "wload", "ystore", "idarr", "sent", "iot", "fill",
-               "k1", "k2", "k3", "tabdone", "wdone", "r1", "r2", "r3", "r4", "yp", "yv"]
+SEMAPHORES = (["idload", "tab0", "tab1", "wload", "ystore", "idarr", "sent", "iot", "fill",
+               "tabdone", "wdone", "sco", "sc", "cpo", "cp", "yp", "yv"]
               + ["arr%d" % s for s in range(3)]
+              + ["to%d" % m for m in range(4)] + ["tr%d" % m for m in range(4)]
               + ["cmp%d" % s for s in range(4)] + ["qo%d" % s for s in range(4)]
               + ["ev%d" % s for s in range(4)] + ["qe%d" % s for s in range(4)]
               + ["z%d%d" % (s, f) for s in range(4) for f in range(4)])
@@ -64,6 +57,7 @@ def rank_program(g, core, T, topo):
     S = T.sem
     A = AluOpType
     COPY = ActivationFunctionType.Copy
+    V, P, C = g.vector, g.tensor, g.scalar
     peers = _peers(cores, rank, topo)
     dst = [cores[j] for j in peers]
     slot = [_peers(cores, j, topo).index(rank) for j in peers]
@@ -77,105 +71,123 @@ def rank_program(g, core, T, topo):
 
     off = -float(1024 * rank + 256)
 
-    g.sync.dma_start(T.idc[:, 0:1], T.tg[0:1, 0:NC]).then_inc(S.idload, 16)
-    g.scalar.dma_start(T.idc[:, 1:2], T.tg[0:1, NC:2 * NC]).then_inc(S.idload, 16)
-    g.sync.dma_start(T.idc[:, 2:3], T.tg[0:1, 2 * NC:3 * NC]).then_inc(S.idload, 16)
-    g.scalar.dma_start(T.tgf[:, :], T.tg[:, :]).then_inc(S.tgload, 16)
-    g.sync.dma_start(T.tabf[:, :], T.tab[:, :]).then_inc(S.tabload, 16)
-    g.scalar.dma_start(T.wf[:, :], T.w[:, :]).then_inc(S.wload, 16)
+    g.sync.dma_start(T.idl[:, OWN, 5:6], T.tg[0:1, 0:NC]).then_inc(S.idload, 16)
+    C.dma_start(T.idl[:, OWN, 6:7], T.tg[0:1, NC:2 * NC]).then_inc(S.idload, 16)
+    g.sync.dma_start(T.idl[:, OWN, 7:8], T.tg[0:1, 2 * NC:3 * NC]).then_inc(S.idload, 16)
+    for h in range(2):
+        g.sync.dma_start(T.tabf[:, 1024 * h:1024 * h + 1024],
+                         T.tab[:, 1024 * h:1024 * h + 1024]).then_inc(S["tab%d" % h], 16)
+    g.sync.dma_start(T.wf[:, :], T.w[:, :]).then_inc(S.wload, 16)
 
     g.iota(T.vb[:, :], [[1, 4]], -256, 4, allow_small_or_imprecise_dtypes=True).then_inc(S.iot, 1)
     g.wait_ge(S.idload, 48)
     idm = [off_bits[:half], off_bits[half:], on_bits[:half]]
     g.remote_dma_fused(
         [RemoteDMATransfer(dst_ids=[did(k)], dma_engine_mask=_mask(idm[k]), remote_sem=S.idarr,
-                           src=T.idc[:, 0:3], dst=T.idl[:, 3 * slot[k]:3 * slot[k] + 3]) for k in range(3)],
+                           src=T.idl[:, OWN, 5:8], dst=T.idl[:, slot[k], 5:8]) for k in range(3)],
         local_sem=S.sent)
     sent = sum(len(m) for m in idm)
 
-    V = g.vector
-    V.memset(T.zero[:, :], 0.0).then_inc(S.fill, 1)
-    V.wait_ge(S.tgload, 16)
-    V.tensor_scalar(T.ka[:, :], T.tgf[:, 0:NC], 1024.0, off, A.mult, A.add).then_inc(S.k1, 1)
-    V.tensor_scalar(T.kb[:, :], T.tgf[:, NC:2 * NC], 4.0, None, A.mult).then_inc(S.k1, 1)
-    V.wait_ge(S.k1, 2)
-    V.tensor_tensor(T.kc[:, :], T.ka[:, :], T.kb[:, :], A.add).then_inc(S.k2, 1)
-    V.wait_ge(S.k2, 1)
-    V.tensor_tensor(T.kown[:, :], T.kc[:, :], T.tgf[:, 2 * NC:3 * NC], A.add).then_inc(S.k3, 1)
-    V.wait_ge(S.k3, 1)
-    V.wait_ge(S.iot, 1)
+    V.memset(T.idl[:, :, 8:40], 0.0).then_inc(S.fill, 1)
+    V.memset(T.d0[:, :], 1.0).then_inc(S.fill, 1)
+    V.wait_ge(S.fill, 2)
+    V.memset(T.idl[:, :, 8:9], off).then_inc(S.fill, 1)
+    V.memset(T.d0[:, 0:1], 0.0).then_inc(S.fill, 1)
+    V.memset(T.d0[:, 1:2], 256.0).then_inc(S.fill, 1)
+    V.memset(T.d0[:, 2:3], 4.0).then_inc(S.fill, 1)
+    V.wait_ge(S.fill, 6)
 
-    def onehot(s, keys):
-        for b in range(4):
-            V.tensor_scalar(T.of[:, 512 * s + b:512 * s + 512:4], keys, T.vb[:, b:b + 1], None,
-                            A.is_equal).then_inc(S["cmp%d" % s], 1)
+    cross = [(m, a) for m in range(4) for a in range(4) if a != m]
+
+    def keys(lo, hi, scan_sem, tr, copy_sem):
+        for s in range(lo, hi):
+            V.tensor_tensor_scan(T.x[:, s, 29:64], T.d0[:, :], T.idl[:, s, 5:40], 0.0, A.mult, A.add).then_inc(scan_sem, 1)
+        V.wait_ge(scan_sem, hi - lo)
+        for m in range(4):
+            q = slice(32 * m, 32 * m + 32)
+            V.transpose(T.key[q, lo:hi, q], T.x[q, lo:hi, 32:64]).then_inc(S["%s%d" % (tr, m)], 1)
+        for queue, pairs in ((C, cross[:4]), (V, cross[4:])):
+            seen = -1
+            for m, a in pairs:
+                if m != seen:
+                    queue.wait_ge(S["%s%d" % (tr, m)], 1)
+                    seen = m
+                q = slice(32 * m, 32 * m + 32)
+                o, n = T.key[32 * a:32 * a + 32, lo:hi, q], T.key[q, lo:hi, q]
+                (V.tensor_copy(o, n) if queue is V else C.activation(o, n, COPY)).then_inc(copy_sem, 1)
+        V.wait_ge(S["%s0" % tr], 1)
+        V.wait_ge(copy_sem, len(cross))
+
+    def compare(s, b):
+        V.tensor_scalar(T.of[:, 512 * s + b:512 * s + 512:4], T.key[:, s, :], T.vb[:, b:b + 1], None,
+                        A.is_equal).then_inc(S["cmp%d" % s], 1)
+
+    def pack_onehot(s):
         V.wait_ge(S["cmp%d" % s], 4)
         V.quantize_mx(T.oq[:, 128 * s:128 * s + 128], T.osc[:, 128 * s:128 * s + 128],
                       T.of[:, 512 * s:512 * s + 512]).then_inc(S["qo%d" % s], 1)
 
-    onehot(3, T.kown[:, :])
-    V.wait_ge(S.tabload, 16)
-    V.quantize_mx(T.tabq[:, :], T.tabs[:, :], T.tabf[:, :]).then_inc(S.tabdone, 1)
-    V.wait_ge(S.wload, 16)
-    V.quantize_mx(T.wq[:, :], T.ws[:, :], T.wf[:, :]).then_inc(S.wdone, 1)
-
-    V.wait_ge(S.fill, 1)
-    V.wait_ge(S.idarr, sum(len(m) for m in idm))
-    V.tensor_scalar(T.u[:, :], T.idl[:, 1:9:3], 4.0, off, A.mult, A.add).then_inc(S.r1, 1)
-    for s in range(3):
-        V.tensor_scalar(T.v[:, s:s + 1], T.idl[:, 3 * s:3 * s + 1], 1024.0, T.idl[:, 3 * s + 2:3 * s + 3],
-                        A.mult, A.add).then_inc(S.r1, 1)
-    V.wait_ge(S.r1, 4)
-    for s in range(3):
-        V.tensor_scalar(T.x[:, 32 * s:32 * s + 32], T.zero[:, :], T.u[:, s:s + 1], T.v[:, s:s + 1],
-                        A.add, A.add).then_inc(S.r2, 1)
-    V.wait_ge(S.r2, 3)
-    for s in range(3):
-        V.transpose(T.xt[:, s:96:3], T.x[:, 32 * s:32 * s + 32]).then_inc(S.r3, 1)
-    V.wait_ge(S.r3, 3)
-    g.scalar.wait_ge(S.r3, 3)
-    spread = [(m, a) for m in range(4) for a in range(4)]
-    for i, (m, a) in enumerate(spread):
-        o = T.key[32 * a:32 * a + 32, 96 * m:96 * m + 96]
-        n = T.xt[32 * m:32 * m + 32, 0:96]
-        if i < 10:
-            V.tensor_copy(o, n).then_inc(S.r4, 1)
-        else:
-            g.scalar.activation(o, n, COPY).then_inc(S.r4, 1)
-    V.wait_ge(S.r4, 16)
-    for s in range(3):
-        onehot(s, T.key[:, s:384:3])
-
-    P = g.tensor
-    P.wait_ge(S.tabdone, 1)
-    order = [0, 1, 2, 3]
-    bank = {0: 0, 1: 4, 2: 0, 3: 4}
+    bank = {0: 0, 1: 4, 2: 0, OWN: 4}
 
     def zview(s, f):
         c = 512 * (bank[s] + f)
         return T.ps[:, c:c + 128]
 
-    for s in order:
+    def lookup(s, before):
         P.wait_ge(S["qo%d" % s], 1)
-        if s >= 2:
-            P.wait_ge(S["ev%d" % (s - 2)], 4)
+        if before is not None:
+            P.wait_ge(S["ev%d" % before], 4)
         for f in range(4):
             P.matmul_mx(zview(s, f), T.tabq[:, 128 * f:128 * f + 128], T.tabs[:, 128 * f:128 * f + 128],
                         T.oq[:, 128 * s:128 * s + 128], T.osc[:, 128 * s:128 * s + 128],
                         True, True).then_inc(S["z%d%d" % (s, f)], 1)
 
-    for s in order:
-        for f in range(4):
-            o = T.ef[:, 512 * s + f:512 * s + 512:4]
-            if s == 0 or f % 2 == 0:
-                g.scalar.wait_ge(S["z%d%d" % (s, f)], 1)
-                g.scalar.activation(o, zview(s, f), COPY).then_inc(S["ev%d" % s], 1)
-            else:
-                V.wait_ge(S["z%d%d" % (s, f)], 1)
-                V.tensor_copy(o, zview(s, f)).then_inc(S["ev%d" % s], 1)
+    def evacuate(queue, s, f):
+        o = T.ef[:, 512 * s + f:512 * s + 512:4]
+        queue.wait_ge(S["z%d%d" % (s, f)], 1)
+        (V.tensor_copy(o, zview(s, f)) if queue is V else C.activation(o, zview(s, f), COPY)).then_inc(S["ev%d" % s], 1)
+
+    def pack_entries(s):
         V.wait_ge(S["ev%d" % s], 4)
         V.quantize_mx(T.eq[:, 128 * s:128 * s + 128], T.esc[:, 128 * s:128 * s + 128],
                       T.ef[:, 512 * s:512 * s + 512]).then_inc(S["qe%d" % s], 1)
+
+    V.wait_ge(S.idload, 48)
+    V.wait_ge(S.iot, 1)
+    keys(OWN, OWN + 1, S.sco, "to", S.cpo)
+    for b in range(4):
+        compare(OWN, b)
+    pack_onehot(OWN)
+    for h in range(2):
+        V.wait_ge(S["tab%d" % h], 16)
+        V.quantize_mx(T.tabq[:, 256 * h:256 * h + 256], T.tabs[:, 256 * h:256 * h + 256],
+                      T.tabf[:, 1024 * h:1024 * h + 1024]).then_inc(S.tabdone, 1)
+    P.wait_ge(S.tabdone, 2)
+    lookup(OWN, None)
+    for f in range(4):
+        evacuate(C, OWN, f)
+
+    V.wait_ge(S.idarr, sum(len(m) for m in idm))
+    keys(0, 3, S.sc, "tr", S.cp)
+    for b in range(4):
+        compare(0, b)
+    for s in range(3):
+        if s < 2:
+            compare(s + 1, 0)
+        pack_onehot(s)
+        if s < 2:
+            for b in range(1, 4):
+                compare(s + 1, b)
+    for s, before in ((0, None), (1, OWN), (2, 0)):
+        lookup(s, before)
+    on_vector = [(1, 1), (1, 3), (2, 3)]
+    for s in range(3):
+        for f in range(4):
+            evacuate(V if (s, f) in on_vector else C, s, f)
+        pack_entries(s)
+    pack_entries(OWN)
+    V.wait_ge(S.wload, 16)
+    V.quantize_mx(T.wq[:, :], T.ws[:, :], T.wf[:, :]).then_inc(S.wdone, 1)
 
     def codes(t, k):
         return t[:, 128 * k:128 * k + 128].bitcast(dt.uint8)
@@ -200,9 +212,9 @@ def rank_program(g, core, T, topo):
     g.wait_ge(S.sent, sent)
 
     P.wait_ge(S.wdone, 1)
-    P.wait_ge(S.qe3, 1)
-    P.wait_ge(S.ev2, 4)
-    out = T.ps[:, 0:128]
+    P.wait_ge(S["qe%d" % OWN], 1)
+    P.wait_ge(S.ev1, 4)
+    out = T.ps[:, 2048:2176]
     P.matmul_mx(out, T.wq[:, :], T.ws[:, :], T.eq[:, 384:512], T.esc[:, 384:512], True, False)
     for i, s in enumerate((0, 2, 1)):
         P.wait_ge(S["arr%d" % s], 2 * len(em[s]))

from concourse.bass import DstId, RemoteDMATransfer
from concourse.mybir import dt, AluOpType, ActivationFunctionType

NC = 128
OWN = 3
SCRATCH = {
    "idl": ("sbuf", [128, 4, 40], "bfloat16"),
    "d0": ("sbuf", [128, 35], "bfloat16"),
    "x": ("sbuf", [128, 4, 64], "bfloat16"),
    "key": ("sbuf", [128, 4, 128], "bfloat16"),
    "tabf": ("sbuf", [128, 2048], "bfloat16"),
    "wf": ("sbuf", [128, 512], "bfloat16"),
    "tabq": ("sbuf", [128, 512], "float8_e4m3fn_x4"),
    "tabs": ("sbuf", [128, 512], "uint8"),
    "wq": ("sbuf", [128, 128], "float8_e4m3fn_x4"),
    "ws": ("sbuf", [128, 128], "uint8"),
    "vb": ("sbuf", [128, 4], "bfloat16"),
    "of": ("sbuf", [128, 2048], "bfloat16"),
    "oq": ("sbuf", [128, 512], "float8_e4m3fn_x4"),
    "osc": ("sbuf", [128, 512], "uint8"),
    "ef": ("sbuf", [128, 2048], "bfloat16"),
    "eq": ("sbuf", [128, 512], "float8_e4m3fn_x4"),
    "esc": ("sbuf", [128, 512], "uint8"),
    "rq": ("sbuf", [128, 384], "float8_e4m3fn_x4"),
    "rs": ("sbuf", [128, 384], "uint8"),
    "yo": ("sbuf", [128, 128], "float32"),
    "ps": ("psum", [128, 4096], "float32"),
}
SEMAPHORES = (["idload", "tab0", "tab1", "wload", "ystore", "idarr", "sent", "iot", "fill",
               "tabdone", "wdone", "sco", "sc", "cpo", "cp", "yp", "yv"]
              + ["arr%d" % s for s in range(3)]
              + ["to%d" % m for m in range(4)] + ["tr%d" % m for m in range(4)]
              + ["cmp%d" % s for s in range(4)] + ["qo%d" % s for s in range(4)]
              + ["ev%d" % s for s in range(4)] + ["qe%d" % s for s in range(4)]
              + ["z%d%d" % (s, f) for s in range(4) for f in range(4)])


def _bits(m):
    return [i for i in range(m.bit_length()) if (m >> i) & 1]


def _mask(b):
    return sum(1 << i for i in b)


def _peers(cores, me, topo):
    def far(j):
        return (topo.chip(cores[j]) == topo.chip(cores[me]), topo.die(cores[j]) == topo.die(cores[me]), j)
    return sorted([j for j in range(len(cores)) if j != me], key=far)


def rank_program(g, core, T, topo):
    rank = T.rank_of(core)
    if rank is None:
        return
    cores = T.cores
    S = T.sem
    A = AluOpType
    COPY = ActivationFunctionType.Copy
    V, P, C = g.vector, g.tensor, g.scalar
    peers = _peers(cores, rank, topo)
    dst = [cores[j] for j in peers]
    slot = [_peers(cores, j, topo).index(rank) for j in peers]
    off_bits = _bits(topo.mask(core, dst[0]))
    on_bits = [b for b in _bits(topo.mask(core, dst[2])) if b not in off_bits]
    half = len(off_bits) // 2

    def did(k):
        rid, pid, _ = topo.addr(dst[k])
        return DstId(rid=rid, pnc=pid)

    off = -float(1024 * rank + 256)

    g.sync.dma_start(T.idl[:, OWN, 5:6], T.tg[0:1, 0:NC]).then_inc(S.idload, 16)
    C.dma_start(T.idl[:, OWN, 6:7], T.tg[0:1, NC:2 * NC]).then_inc(S.idload, 16)
    g.sync.dma_start(T.idl[:, OWN, 7:8], T.tg[0:1, 2 * NC:3 * NC]).then_inc(S.idload, 16)
    for h in range(2):
        g.sync.dma_start(T.tabf[:, 1024 * h:1024 * h + 1024],
                         T.tab[:, 1024 * h:1024 * h + 1024]).then_inc(S["tab%d" % h], 16)
    g.sync.dma_start(T.wf[:, :], T.w[:, :]).then_inc(S.wload, 16)

    g.iota(T.vb[:, :], [[1, 4]], -256, 4, allow_small_or_imprecise_dtypes=True).then_inc(S.iot, 1)
    g.wait_ge(S.idload, 48)
    idm = [off_bits[:half], off_bits[half:], on_bits[:half]]
    g.remote_dma_fused(
        [RemoteDMATransfer(dst_ids=[did(k)], dma_engine_mask=_mask(idm[k]), remote_sem=S.idarr,
                           src=T.idl[:, OWN, 5:8], dst=T.idl[:, slot[k], 5:8]) for k in range(3)],
        local_sem=S.sent)
    sent = sum(len(m) for m in idm)

    V.memset(T.idl[:, :, 8:40], 0.0).then_inc(S.fill, 1)
    V.memset(T.d0[:, :], 1.0).then_inc(S.fill, 1)
    V.wait_ge(S.fill, 2)
    V.memset(T.idl[:, :, 8:9], off).then_inc(S.fill, 1)
    V.memset(T.d0[:, 0:1], 0.0).then_inc(S.fill, 1)
    V.memset(T.d0[:, 1:2], 256.0).then_inc(S.fill, 1)
    V.memset(T.d0[:, 2:3], 4.0).then_inc(S.fill, 1)
    V.wait_ge(S.fill, 6)

    cross = [(m, a) for m in range(4) for a in range(4) if a != m]

    def keys(lo, hi, scan_sem, tr, copy_sem):
        for s in range(lo, hi):
            V.tensor_tensor_scan(T.x[:, s, 29:64], T.d0[:, :], T.idl[:, s, 5:40], 0.0, A.mult, A.add).then_inc(scan_sem, 1)
        V.wait_ge(scan_sem, hi - lo)
        for m in range(4):
            q = slice(32 * m, 32 * m + 32)
            V.transpose(T.key[q, lo:hi, q], T.x[q, lo:hi, 32:64]).then_inc(S["%s%d" % (tr, m)], 1)
        for queue, pairs in ((C, cross[:4]), (V, cross[4:])):
            seen = -1
            for m, a in pairs:
                if m != seen:
                    queue.wait_ge(S["%s%d" % (tr, m)], 1)
                    seen = m
                q = slice(32 * m, 32 * m + 32)
                o, n = T.key[32 * a:32 * a + 32, lo:hi, q], T.key[q, lo:hi, q]
                (V.tensor_copy(o, n) if queue is V else C.activation(o, n, COPY)).then_inc(copy_sem, 1)
        V.wait_ge(S["%s0" % tr], 1)
        V.wait_ge(copy_sem, len(cross))

    def compare(s, b):
        V.tensor_scalar(T.of[:, 512 * s + b:512 * s + 512:4], T.key[:, s, :], T.vb[:, b:b + 1], None,
                        A.is_equal).then_inc(S["cmp%d" % s], 1)

    def pack_onehot(s):
        V.wait_ge(S["cmp%d" % s], 4)
        V.quantize_mx(T.oq[:, 128 * s:128 * s + 128], T.osc[:, 128 * s:128 * s + 128],
                      T.of[:, 512 * s:512 * s + 512]).then_inc(S["qo%d" % s], 1)

    bank = {0: 0, 1: 4, 2: 0, OWN: 4}

    def zview(s, f):
        c = 512 * (bank[s] + f)
        return T.ps[:, c:c + 128]

    def lookup(s, before):
        P.wait_ge(S["qo%d" % s], 1)
        if before is not None:
            P.wait_ge(S["ev%d" % before], 4)
        for f in range(4):
            P.matmul_mx(zview(s, f), T.tabq[:, 128 * f:128 * f + 128], T.tabs[:, 128 * f:128 * f + 128],
                        T.oq[:, 128 * s:128 * s + 128], T.osc[:, 128 * s:128 * s + 128],
                        True, True).then_inc(S["z%d%d" % (s, f)], 1)

    def evacuate(queue, s, f):
        o = T.ef[:, 512 * s + f:512 * s + 512:4]
        queue.wait_ge(S["z%d%d" % (s, f)], 1)
        (V.tensor_copy(o, zview(s, f)) if queue is V else C.activation(o, zview(s, f), COPY)).then_inc(S["ev%d" % s], 1)

    def pack_entries(s):
        V.wait_ge(S["ev%d" % s], 4)
        V.quantize_mx(T.eq[:, 128 * s:128 * s + 128], T.esc[:, 128 * s:128 * s + 128],
                      T.ef[:, 512 * s:512 * s + 512]).then_inc(S["qe%d" % s], 1)

    V.wait_ge(S.idload, 48)
    V.wait_ge(S.iot, 1)
    keys(OWN, OWN + 1, S.sco, "to", S.cpo)
    for b in range(4):
        compare(OWN, b)
    pack_onehot(OWN)
    for h in range(2):
        V.wait_ge(S["tab%d" % h], 16)
        V.quantize_mx(T.tabq[:, 256 * h:256 * h + 256], T.tabs[:, 256 * h:256 * h + 256],
                      T.tabf[:, 1024 * h:1024 * h + 1024]).then_inc(S.tabdone, 1)
    P.wait_ge(S.tabdone, 2)
    lookup(OWN, None)
    for f in range(4):
        evacuate(C, OWN, f)

    V.wait_ge(S.idarr, sum(len(m) for m in idm))
    keys(0, 3, S.sc, "tr", S.cp)
    for b in range(4):
        compare(0, b)
    for s in range(3):
        if s < 2:
            compare(s + 1, 0)
        pack_onehot(s)
        if s < 2:
            for b in range(1, 4):
                compare(s + 1, b)
    for s, before in ((0, None), (1, OWN), (2, 0)):
        lookup(s, before)
    on_vector = [(1, 1), (1, 3), (2, 3)]
    for s in range(3):
        for f in range(4):
            evacuate(V if (s, f) in on_vector else C, s, f)
        pack_entries(s)
    pack_entries(OWN)
    V.wait_ge(S.wload, 16)
    V.quantize_mx(T.wq[:, :], T.ws[:, :], T.wf[:, :]).then_inc(S.wdone, 1)

    def codes(t, k):
        return t[:, 128 * k:128 * k + 128].bitcast(dt.uint8)

    def scales(t, k):
        return t[:, 128 * k:128 * k + 128]

    em = [off_bits, off_bits, on_bits]
    rid0, pid0, _ = topo.addr(dst[0])
    g.wait_ge(S.qe0, 1)
    for part, src, land in ((codes, T.eq, T.rq), (scales, T.esc, T.rs)):
        g.remote_dma(part(land, slot[0]), part(src, 0), S["arr%d" % slot[0]], S.sent, pid0, rid0, _mask(em[0]))
        sent += len(em[0])
    g.wait_ge(S.qe1, 1)
    g.wait_ge(S.qe2, 1)
    for part, src, land in ((codes, T.eq, T.rq), (scales, T.esc, T.rs)):
        g.remote_dma_fused(
            [RemoteDMATransfer(dst_ids=[did(k)], dma_engine_mask=_mask(em[k]), remote_sem=S["arr%d" % slot[k]],
                               src=part(src, k), dst=part(land, slot[k])) for k in (1, 2)],
            local_sem=S.sent)
        sent += len(em[1]) + len(em[2])
    g.wait_ge(S.sent, sent)

    P.wait_ge(S.wdone, 1)
    P.wait_ge(S["qe%d" % OWN], 1)
    P.wait_ge(S.ev1, 4)
    out = T.ps[:, 2048:2176]
    P.matmul_mx(out, T.wq[:, :], T.ws[:, :], T.eq[:, 384:512], T.esc[:, 384:512], True, False)
    for i, s in enumerate((0, 2, 1)):
        P.wait_ge(S["arr%d" % s], 2 * len(em[s]))
        m = P.matmul_mx(out, T.wq[:, :], T.ws[:, :], T.rq[:, 128 * s:128 * s + 128], T.rs[:, 128 * s:128 * s + 128],
                        False, i == 2)
    m.then_inc(S.yp, 1)
    V.wait_ge(S.yp, 1)
    V.tensor_copy(T.yo[:, :], out).then_inc(S.yv, 1)
    g.sync.wait_ge(S.yv, 1)
    g.sync.dma_start(T.y[:, :], T.yo[:, :]).then_inc(S.ystore, 16)
    g.sync.wait_ge(S.ystore, 16)
